import numpy as np
import ml_dtypes


def mxq(x, axis, fmt="e4m3"):
    dtype, down = {"e4m3": (ml_dtypes.float8_e4m3fn, 7), "e5m2": (ml_dtypes.float8_e5m2, 14)}[fmt]
    v = np.moveaxis(np.asarray(x, np.float32).astype(ml_dtypes.bfloat16).astype(np.float64), axis, -1)
    blocks = v.reshape(v.shape[:-1] + (-1, 32))
    amax = np.abs(blocks).max(-1, keepdims=True)
    byte = np.maximum(np.where(amax > 0, np.frexp(amax)[1] - 1 + 127, 0) - down, 1)
    scale = np.exp2(byte - 127.0)
    codes = (blocks / scale).astype(np.float32).astype(dtype).astype(np.float64)
    return np.moveaxis((codes * scale).reshape(v.shape), -1, axis)


WIDE = False


def mx_kscale(k):
    if not WIDE:
        return np.ones(k)
    levels = np.array([30, -30])
    if k % 512:
        return np.exp2(np.random.permutation(np.resize(levels, k // 32))).repeat(32)
    a = np.empty((k // 512, 16))
    for p in range(k // 512):
        a[p, :8] = np.random.permutation(np.resize(levels, 8))
        for g in range(8):
            far = levels[np.abs(levels - a[p, g]) >= 10]
            a[p, g + 8] = far[np.random.randint(len(far))]
    return np.exp2(a.ravel()).repeat(32)


def f64(x):
    return np.asarray(x).astype(np.float64)


def striped(idx):
    return np.tile(np.asarray(idx).reshape(-1, 16).T, (8, 1)).astype(np.uint16)


def unstriped(offs):
    return offs[:16].T.reshape(-1).astype(np.int64)


E2M1 = np.array([0.0, 0.5, 1.0, 1.5, 2.0, 3.0, 4.0, 6.0, -0.0, -0.5, -1.0, -1.5, -2.0, -3.0, -4.0, -6.0])


def pack_weight(w, fmt):
    k, n = w.shape
    w = f64(np.asarray(w, np.float32).astype(ml_dtypes.bfloat16)).reshape(k // 32, 32, n)
    amax = np.abs(w).max(1)
    if fmt == "e4m3":
        byte = np.frexp(amax)[1] - 1 + 127 - 7
    else:
        mant, ex = np.frexp(amax / 6.0)
        byte = np.where(mant > 0.5, ex, ex - 1) + 127
    byte = np.clip(np.where(amax > 0, byte, 1), 1, 254)
    scaled = (w * np.exp2(127.0 - byte)[:, None, :]).reshape(k, n).astype(np.float32)
    by_word = np.ascontiguousarray(scaled.reshape(k // 512, 128, 4, n).transpose(0, 1, 3, 2))
    if fmt == "e4m3":
        words = by_word.astype(ml_dtypes.float8_e4m3fn).view(np.uint8)
    else:
        c = by_word.astype(ml_dtypes.float4_e2m1fn).view(np.uint8) & 0xF
        words = (c[..., 0::2] | (c[..., 1::2] << 4)).reshape(k // 512, 128, 2 * n)
    return np.ascontiguousarray(words), np.ascontiguousarray(byte.astype(np.uint8).reshape(k // 512, 16, n))


def unpack_weight(words, scales, fmt):
    g, _, n = scales.shape
    words = np.ascontiguousarray(words).reshape(g, 128, n, -1)
    if fmt == "e4m3":
        vals = words.view(ml_dtypes.float8_e4m3fn).astype(np.float64)
    else:
        nib = np.empty((g, 128, n, 4), np.uint8)
        nib[..., 0::2] = words & 0xF
        nib[..., 1::2] = words >> 4
        vals = E2M1[nib]
    vals = vals * np.repeat(np.exp2(scales.astype(np.float64) - 127.0), 8, axis=1)[..., None]
    return vals.transpose(0, 1, 3, 2).reshape(g * 512, n)


K, T, J, I, L, S, R, N = 512, 1024, 256, 128, 128, 512, 512, 256


def setup_inputs():
    n = np.random.standard_normal
    idx = np.random.permutation(T)[:I]
    idx2 = np.random.permutation(S)[:L]
    fk = mx_kscale(K)
    fr = mx_kscale(R)
    wbp = pack_weight(n((R, N)) * 1 / np.sqrt(R) / fr[:, None], "e2m1")
    return {
        "xa": (n((K, T)) / fk[:, None]).astype(np.float32),
        "xb": (n((K, S)) * 0.6 / fk[:, None]).astype(np.float32),
        "w": (n((K, R)) * 1 / np.sqrt(K) * fk[:, None] * fr).astype(np.float32),
        "wb_words": wbp[0],
        "wb_scales": wbp[1],
        "rs": (n((N, J))).astype(np.float32),
        "offs": striped(idx),
        "offs2": striped(idx2),
    }


def reference(xa, xb, w, wb_words, wb_scales, rs, offs, offs2):
    idx = unstriped(offs)
    idx2 = unstriped(offs2)
    wbu = unpack_weight(wb_words, wb_scales, "e2m1")
    u = np.concatenate([f64(xa)[:, idx], f64(xb)[:, idx2]], axis=1)
    wq = mxq(f64(w), 0, "e5m2")
    uq = mxq(u, 0, "e4m3")
    a = wq.T @ uq
    hid = np.maximum(a, 0.0)
    hidq = mxq(hid, 0, "e5m2")
    p = wbu.T @ hidq
    p1 = np.pad(p, ((0, 0), (1, 0)))[:, :J]
    y = p - 0.7 * p1 + 0.5 * f64(rs)
    return y

@@ -1,0 +1,158 @@
+from contextlib import ExitStack
+
+import concourse.mybir as mybir
+
+K, T, S, R, N, J = 512, 1024, 512, 512, 256, 256
+FLOPS = 2 * K * R * J + 2 * R * N * J
+
+F32 = mybir.dt.float32
+BF16 = mybir.dt.bfloat16
+I32 = mybir.dt.int32
+U32 = mybir.dt.uint32
+U16 = mybir.dt.uint16
+U8 = mybir.dt.uint8
+E4M3 = mybir.dt.float8_e4m3fn_x4
+E5M2 = mybir.dt.float8_e5m2_x4
+E2M1 = mybir.dt.float4_e2m1fn_x4
+MULT = mybir.AluOpType.mult
+ADD = mybir.AluOpType.add
+COPY = mybir.ActivationFunctionType.Copy
+RELU = mybir.ActivationFunctionType.Relu
+
+P = 128
+PACK = 4
+HALF = 128
+GROUPS = N // P
+LAG = -0.7
+RES = 0.5
+EARLY = HALF + 8
+
+
+def tile_list_joined_plain_lagged_kernel(tc, xa, xb, w, wb_words, wb_scales, rs, offs, offs2, out):
+    nc = tc.nc
+    with ExitStack() as ctx:
+        sb = ctx.enter_context(tc.tile_pool(name="sb", bufs=1))
+        ps = ctx.enter_context(tc.psum_pool(name="ps", bufs=1))
+
+        list_a = sb.tile([P, HALF // 16], U16, name="list_a")
+        list_b = sb.tile([P, HALF // 16], U16, name="list_b")
+        w_raw = sb.tile([P, PACK, R], F32, name="w_raw")
+        xb_raw = sb.tile([P, PACK, S], F32, name="xb_raw")
+        xa_01 = sb.tile([P, 2, T], F32, name="xa_01")
+        xa_2 = sb.tile([P, T], F32, name="xa_2")
+        xa_3 = sb.tile([P, T], F32, name="xa_3")
+        wb_codes = sb.tile([P, 2 * N], U8, name="wb_codes", align_bytes=64)
+        wb_plane = sb.tile([P, N], U8, name="wb_plane", align_bytes=64)
+        rs_raw = sb.tile([P, GROUPS, J], F32, name="rs_raw")
+        res = sb.tile([P, GROUPS, J], F32, name="res")
+
+        nc.vector.memset(wb_plane[:].bitcast(U32), 0)
+        xa_rows = xa.rearrange("(p t) c -> p t c", t=PACK)
+        nc.sync.dma_start(out=w_raw[:], in_=w.rearrange("(p t) r -> p t r", t=PACK))
+        for q in range(4):
+            nc.sync.dma_start(
+                out=wb_plane[32 * q : 32 * q + 4, :].bitcast(I32),
+                in_=wb_scales[0, 4 * q : 4 * q + 4, :].bitcast(I32),
+            )
+        nc.sync.dma_start(list_b[:], offs2)
+        nc.sync.dma_start(list_a[:], offs)
+        nc.sync.dma_start(out=xb_raw[:], in_=xb.rearrange("(p t) c -> p t c", t=PACK))
+        nc.sync.dma_start(out=xa_01[:], in_=xa_rows[:, 0:2, :])
+        nc.sync.dma_start(out=xa_2[:], in_=xa_rows[:, 2, :])
+        nc.sync.dma_start(out=xa_3[:], in_=xa_rows[:, 3, :])
+        nc.sync.dma_start(out=wb_codes[:].bitcast(I32), in_=wb_words[0].bitcast(I32))
+        nc.sync.dma_start(out=rs_raw[:], in_=rs.rearrange("(g p) j -> p g j", p=P))
+
+        w_codes = []
+        w_planes = []
+        for h in range(2):
+            w_bf = sb.tile([P, 2, P, PACK], BF16, name=f"w_bf{h}", align_bytes=64)
+            src = w_raw[:].rearrange("p t (m u) -> p m t u", u=PACK)[:, :, :, 2 * h : 2 * h + 2]
+            dst = w_bf[:].rearrange("p u m t -> p m t u")
+            if h == 0:
+                nc.vector.tensor_copy(out=dst, in_=src)
+            else:
+                nc.scalar.activation(out=dst, in_=src, func=COPY)
+            codes = sb.tile([P, 2 * P], U32, name=f"w_codes{h}", align_bytes=64)
+            plane = sb.tile([P, 2 * P], U8, name=f"w_plane{h}", align_bytes=64)
+            nc.vector.quantize_mx(
+                out=codes[:].bitcast(E5M2), scales=plane[:], in_=w_bf[:].rearrange("p u m t -> p (u m t)")
+            )
+            w_codes.append(codes)
+            w_planes.append(plane)
+
+        def two_layers(name, windows, offsets, p_banks):
+            u_bf = sb.tile([P, HALF, PACK], BF16, name=f"u_bf_{name}", align_bytes=64)
+            for t in range(PACK):
+                nc.vector.tensor_copy(out=u_bf[:, :, t], in_=windows[t].indirect(offsets[:]))
+            u_codes = sb.tile([P, HALF], U32, name=f"u_codes_{name}", align_bytes=64)
+            u_plane = sb.tile([P, HALF], U8, name=f"u_plane_{name}", align_bytes=64)
+            nc.vector.quantize_mx(
+                out=u_codes[:].bitcast(E4M3), scales=u_plane[:], in_=u_bf[:].rearrange("p j t -> p (j t)")
+            )
+            a_bank = ps.tile([P, PACK, HALF], F32, name=f"a_bank_{name}")
+            for u in range(PACK):
+                cols = slice((u % 2) * P, (u % 2 + 1) * P)
+                nc.tensor.matmul_mx(
+                    out=a_bank[:, u, :],
+                    lhsT=w_codes[u // 2][:, cols].bitcast(E5M2),
+                    lhsT_scale=w_planes[u // 2][:, cols],
+                    rhs=u_codes[:].bitcast(E4M3),
+                    rhs_scale=u_plane[:],
+                    start=True,
+                    stop=True,
+                )
+            h_bf = sb.tile([P, HALF, PACK], BF16, name=f"h_bf_{name}", align_bytes=64)
+            nc.scalar.activation(out=h_bf[:], in_=a_bank[:].rearrange("p u j -> p j u"), func=RELU)
+            h_codes = sb.tile([P, HALF], U32, name=f"h_codes_{name}", align_bytes=64)
+            h_plane = sb.tile([P, HALF], U8, name=f"h_plane_{name}", align_bytes=64)
+            nc.vector.quantize_mx(
+                out=h_codes[:].bitcast(E5M2), scales=h_plane[:], in_=h_bf[:].rearrange("p j t -> p (j t)")
+            )
+            for g in range(GROUPS):
+                nc.tensor.matmul_mx(
+                    out=p_banks[g],
+                    lhsT=wb_codes[:, 2 * P * g : 2 * P * (g + 1)].bitcast(E2M1),
+                    lhsT_scale=wb_plane[:, P * g : P * (g + 1)],
+                    rhs=h_codes[:].bitcast(E5M2),
+                    rhs_scale=h_plane[:],
+                    start=True,
+                    stop=True,
+                )
+
+        out_rows = out.rearrange("(g p) j -> p g j", p=P)
+
+        p_b = ps.tile([P, GROUPS, HALF], F32, name="p_b")
+        two_layers("b", [xb_raw[:, t, :] for t in range(PACK)], list_b, [p_b[:, g, :] for g in range(GROUPS)])
+
+        p_a = [ps.tile([P, HALF], F32, name=f"p_a{g}") for g in range(GROUPS)]
+        two_layers("a", [xa_01[:, 0, :], xa_01[:, 1, :], xa_2[:], xa_3[:]], list_a, [bank[:] for bank in p_a])
+
+        nc.vector.scalar_tensor_tensor(
+            out=res[:, :, HALF:J], in0=rs_raw[:, :, HALF:J], scalar=RES, in1=p_b[:], op0=MULT, op1=ADD
+        )
+        nc.vector.scalar_tensor_tensor(
+            out=res[:, :, HALF + 1 : J],
+            in0=p_b[:, :, 0 : HALF - 1],
+            scalar=LAG,
+            in1=res[:, :, HALF + 1 : J],
+            op0=MULT,
+            op1=ADD,
+        )
+        nc.sync.dma_start(out=out_rows[:, :, EARLY:J], in_=res[:, :, EARLY:J])
+
+        for g in range(GROUPS):
+            nc.vector.scalar_tensor_tensor(
+                out=res[:, g, 0:HALF], in0=rs_raw[:, g, 0:HALF], scalar=RES, in1=p_a[g][:], op0=MULT, op1=ADD
+            )
+        for g in range(GROUPS):
+            nc.vector.scalar_tensor_tensor(
+                out=res[:, g, 1 : HALF + 1],
+                in0=p_a[g][:],
+                scalar=LAG,
+                in1=res[:, g, 1 : HALF + 1],
+                op0=MULT,
+                op1=ADD,
+            )
+            queue = nc.sync if g == 0 else nc.scalar
+            queue.dma_start(out=out_rows[:, g, 0:EARLY], in_=res[:, g, 0:EARLY])

@@ -81,20 +81,21 @@ def tile_list_joined_plain_lagged_kernel(tc, xa, xb, w, wb_words, wb_scales, rs,
             w_codes.append(codes)
             w_planes.append(plane)
 
-        def two_layers(name, windows, offsets, p_banks):
+        def two_layers(name, windows, offsets, p_banks, parts, tags):
             u_bf = sb.tile([P, HALF, PACK], BF16, name=f"u_bf_{name}", align_bytes=64)
             for t in range(PACK):
                 nc.vector.tensor_copy(out=u_bf[:, :, t], in_=windows[t].indirect(offsets[:]))
-            u_codes = sb.tile([P, HALF], U32, name=f"u_codes_{name}", align_bytes=64)
+            u_codes = sb.tile([P, HALF], U32, name=f"u_codes_{name}", tag=tags[0], align_bytes=64)
             u_plane = sb.tile([P, HALF], U8, name=f"u_plane_{name}", align_bytes=64)
             nc.vector.quantize_mx(
                 out=u_codes[:].bitcast(E4M3), scales=u_plane[:], in_=u_bf[:].rearrange("p j t -> p (j t)")
             )
-            a_bank = ps.tile([P, PACK, HALF], F32, name=f"a_bank_{name}")
+            width = PACK // parts
+            a_banks = [ps.tile([P, width, HALF], F32, name=f"a_bank_{name}{i}") for i in range(parts)]
             for u in range(PACK):
                 cols = slice((u % 2) * P, (u % 2 + 1) * P)
                 nc.tensor.matmul_mx(
-                    out=a_bank[:, u, :],
+                    out=a_banks[u // width][:, u % width, :],
                     lhsT=w_codes[u // 2][:, cols].bitcast(E5M2),
                     lhsT_scale=w_planes[u // 2][:, cols],
                     rhs=u_codes[:].bitcast(E4M3),
@@ -103,8 +104,14 @@ def tile_list_joined_plain_lagged_kernel(tc, xa, xb, w, wb_words, wb_scales, rs,
                     stop=True,
                 )
             h_bf = sb.tile([P, HALF, PACK], BF16, name=f"h_bf_{name}", align_bytes=64)
-            nc.scalar.activation(out=h_bf[:], in_=a_bank[:].rearrange("p u j -> p j u"), func=RELU)
-            h_codes = sb.tile([P, HALF], U32, name=f"h_codes_{name}", align_bytes=64)
+            for i in range(parts):
+                dst = h_bf[:, :, i * width : (i + 1) * width]
+                src = a_banks[i][:].rearrange("p u j -> p j u")
+                if i == parts - 1:
+                    nc.scalar.activation(out=dst, in_=src, func=RELU)
+                else:
+                    nc.vector.tensor_scalar_max(out=dst, in0=src, scalar1=0.0)
+            h_codes = sb.tile([P, HALF], U32, name=f"h_codes_{name}", tag=tags[1], align_bytes=64)
             h_plane = sb.tile([P, HALF], U8, name=f"h_plane_{name}", align_bytes=64)
             nc.vector.quantize_mx(
                 out=h_codes[:].bitcast(E5M2), scales=h_plane[:], in_=h_bf[:].rearrange("p j t -> p (j t)")
@@ -123,10 +130,10 @@ def tile_list_joined_plain_lagged_kernel(tc, xa, xb, w, wb_words, wb_scales, rs,
         out_rows = out.rearrange("(g p) j -> p g j", p=P)
 
         p_b = ps.tile([P, GROUPS, HALF], F32, name="p_b")
-        two_layers("b", [xb_raw[:, t, :] for t in range(PACK)], list_b, [p_b[:, g, :] for g in range(GROUPS)])
+        two_layers("b", [xb_raw[:, t, :] for t in range(PACK)], list_b, [p_b[:, g, :] for g in range(GROUPS)], 1, ("codes0", "codes1"))
 
         p_a = [ps.tile([P, HALF], F32, name=f"p_a{g}") for g in range(GROUPS)]
-        two_layers("a", [xa_01[:, 0, :], xa_01[:, 1, :], xa_2[:], xa_3[:]], list_a, [bank[:] for bank in p_a])
+        two_layers("a", [xa_01[:, 0, :], xa_01[:, 1, :], xa_2[:], xa_3[:]], list_a, [bank[:] for bank in p_a], 2, ("codes1", "codes0"))
 
         nc.vector.scalar_tensor_tensor(
             out=res[:, :, HALF:J], in0=rs_raw[:, :, HALF:J], scalar=RES, in1=p_b[:], op0=MULT, op1=ADD

@@ -39,7 +39,7 @@ def tile_list_joined_plain_lagged_kernel(tc, xa, xb, w, wb_words, wb_scales, rs,
         w_raw = sb.tile([P, PACK, R], F32, name="w_raw")
         xb_raw = sb.tile([P, PACK, S], F32, name="xb_raw")
         xa_01 = sb.tile([P, 2, T], F32, name="xa_01")
-        xa_2 = sb.tile([P, T], F32, name="xa_2")
+        xa_2 = sb.tile([P, T], F32, name="xa_2", tag="shared_plane", align_bytes=64)
         xa_3 = sb.tile([P, T], F32, name="xa_3")
         wb_codes = sb.tile([P, 2 * N], U8, name="wb_codes", align_bytes=64)
         wb_plane = sb.tile([P, N], U8, name="wb_plane", align_bytes=64)
@@ -48,105 +48,133 @@ def tile_list_joined_plain_lagged_kernel(tc, xa, xb, w, wb_words, wb_scales, rs,
 
         nc.vector.memset(wb_plane[:].bitcast(U32), 0)
         xa_rows = xa.rearrange("(p t) c -> p t c", t=PACK)
-        nc.sync.dma_start(out=w_raw[:], in_=w.rearrange("(p t) r -> p t r", t=PACK))
-        for q in range(4):
-            nc.sync.dma_start(
-                out=wb_plane[32 * q : 32 * q + 4, :].bitcast(I32),
-                in_=wb_scales[0, 4 * q : 4 * q + 4, :].bitcast(I32),
-            )
-        nc.sync.dma_start(list_b[:], offs2)
-        nc.sync.dma_start(list_a[:], offs)
-        nc.sync.dma_start(out=xb_raw[:], in_=xb.rearrange("(p t) c -> p t c", t=PACK))
+
+        def load_w():
+            nc.sync.dma_start(out=w_raw[:], in_=w.rearrange("(p t) r -> p t r", t=PACK))
+
+        def load_xb():
+            nc.sync.dma_start(out=xb_raw[:], in_=xb.rearrange("(p t) c -> p t c", t=PACK))
+
+        def load_lists():
+            nc.sync.dma_start(list_b[:], offs2)
+            nc.sync.dma_start(list_a[:], offs)
+
+        def load_scales():
+            for q in range(4):
+                nc.sync.dma_start(
+                    out=wb_plane[32 * q : 32 * q + 4, :].bitcast(I32),
+                    in_=wb_scales[0, 4 * q : 4 * q + 4, :].bitcast(I32),
+                )
+
+        load_xb()
+        load_lists()
+        load_scales()
+        load_w()
         nc.sync.dma_start(out=xa_01[:], in_=xa_rows[:, 0:2, :])
+        nc.sync.dma_start(out=wb_codes[:].bitcast(I32), in_=wb_words[0].bitcast(I32))
         nc.sync.dma_start(out=xa_2[:], in_=xa_rows[:, 2, :])
         nc.sync.dma_start(out=xa_3[:], in_=xa_rows[:, 3, :])
-        nc.sync.dma_start(out=wb_codes[:].bitcast(I32), in_=wb_words[0].bitcast(I32))
         nc.sync.dma_start(out=rs_raw[:], in_=rs.rearrange("(g p) j -> p g j", p=P))
 
-        w_codes = []
-        w_planes = []
-        for h in range(2):
-            w_bf = sb.tile([P, 2, P, PACK], BF16, name=f"w_bf{h}", align_bytes=64)
-            src = w_raw[:].rearrange("p t (m u) -> p m t u", u=PACK)[:, :, :, 2 * h : 2 * h + 2]
-            dst = w_bf[:].rearrange("p u m t -> p m t u")
-            if h == 0:
-                nc.vector.tensor_copy(out=dst, in_=src)
-            else:
-                nc.scalar.activation(out=dst, in_=src, func=COPY)
-            codes = sb.tile([P, 2 * P], U32, name=f"w_codes{h}", align_bytes=64)
-            plane = sb.tile([P, 2 * P], U8, name=f"w_plane{h}", align_bytes=64)
-            nc.vector.quantize_mx(
-                out=codes[:].bitcast(E5M2), scales=plane[:], in_=w_bf[:].rearrange("p u m t -> p (u m t)")
-            )
-            w_codes.append(codes)
-            w_planes.append(plane)
+        def quantise(name, values, fmt, codes_tag, plane_tag):
+            width = values.shape[1] // PACK
+            codes = sb.tile([P, width], U32, name=f"{name}_codes", tag=codes_tag, align_bytes=64)
+            plane = sb.tile([P, width], U8, name=f"{name}_plane", tag=plane_tag, align_bytes=64)
+            nc.vector.quantize_mx(out=codes[:].bitcast(fmt), scales=plane[:], in_=values)
+            return codes, plane
 
-        def two_layers(name, windows, offsets, p_banks, parts, tags):
-            u_bf = sb.tile([P, HALF, PACK], BF16, name=f"u_bf_{name}", align_bytes=64)
-            for t in range(PACK):
-                nc.vector.tensor_copy(out=u_bf[:, :, t], in_=windows[t].indirect(offsets[:]))
-            u_codes = sb.tile([P, HALF], U32, name=f"u_codes_{name}", tag=tags[0], align_bytes=64)
-            u_plane = sb.tile([P, HALF], U8, name=f"u_plane_{name}", align_bytes=64)
-            nc.vector.quantize_mx(
-                out=u_codes[:].bitcast(E4M3), scales=u_plane[:], in_=u_bf[:].rearrange("p j t -> p (j t)")
-            )
+        def gather(u_bf, t, window, offsets):
+            nc.vector.tensor_copy(out=u_bf[:, :, t], in_=window.indirect(offsets[:]))
+
+        def first_layer(name, u_q, parts):
             width = PACK // parts
-            a_banks = [ps.tile([P, width, HALF], F32, name=f"a_bank_{name}{i}") for i in range(parts)]
+            banks = [ps.tile([P, width, HALF], F32, name=f"a_bank_{name}{i}") for i in range(parts)]
             for u in range(PACK):
                 cols = slice((u % 2) * P, (u % 2 + 1) * P)
                 nc.tensor.matmul_mx(
-                    out=a_banks[u // width][:, u % width, :],
-                    lhsT=w_codes[u // 2][:, cols].bitcast(E5M2),
-                    lhsT_scale=w_planes[u // 2][:, cols],
-                    rhs=u_codes[:].bitcast(E4M3),
-                    rhs_scale=u_plane[:],
+                    out=banks[u // width][:, u % width, :],
+                    lhsT=w_q[u // 2][0][:, cols].bitcast(E5M2),
+                    lhsT_scale=w_q[u // 2][1][:, cols],
+                    rhs=u_q[0][:].bitcast(E4M3),
+                    rhs_scale=u_q[1][:],
                     start=True,
                     stop=True,
                 )
             h_bf = sb.tile([P, HALF, PACK], BF16, name=f"h_bf_{name}", align_bytes=64)
             for i in range(parts):
                 dst = h_bf[:, :, i * width : (i + 1) * width]
-                src = a_banks[i][:].rearrange("p u j -> p j u")
+                src = banks[i][:].rearrange("p u j -> p j u")
                 if i == parts - 1:
                     nc.scalar.activation(out=dst, in_=src, func=RELU)
                 else:
                     nc.vector.tensor_scalar_max(out=dst, in0=src, scalar1=0.0)
-            h_codes = sb.tile([P, HALF], U32, name=f"h_codes_{name}", tag=tags[1], align_bytes=64)
-            h_plane = sb.tile([P, HALF], U8, name=f"h_plane_{name}", align_bytes=64)
-            nc.vector.quantize_mx(
-                out=h_codes[:].bitcast(E5M2), scales=h_plane[:], in_=h_bf[:].rearrange("p j t -> p (j t)")
-            )
+            return h_bf[:].rearrange("p j t -> p (j t)")
+
+        def second_layer(h_q, p_banks):
             for g in range(GROUPS):
                 nc.tensor.matmul_mx(
                     out=p_banks[g],
                     lhsT=wb_codes[:, 2 * P * g : 2 * P * (g + 1)].bitcast(E2M1),
                     lhsT_scale=wb_plane[:, P * g : P * (g + 1)],
-                    rhs=h_codes[:].bitcast(E5M2),
-                    rhs_scale=h_plane[:],
+                    rhs=h_q[0][:].bitcast(E5M2),
+                    rhs_scale=h_q[1][:],
                     start=True,
                     stop=True,
                 )
 
-        out_rows = out.rearrange("(g p) j -> p g j", p=P)
+        ub_bf = sb.tile([P, HALF, PACK], BF16, name="ub_bf", align_bytes=64)
+        for t in range(PACK):
+            gather(ub_bf, t, xb_raw[:, t, :], list_b)
+        ub_q = quantise("ub", ub_bf[:].rearrange("p j t -> p (j t)"), E4M3, "codes0", "ub_plane")
 
+        w_q = []
+        for h in range(2):
+            w_bf = sb.tile([P, 2, P, PACK], BF16, name=f"w_bf{h}", tag=f"rounded{h}", align_bytes=64)
+            src = w_raw[:].rearrange("p t (m u) -> p m t u", u=PACK)[:, :, :, 2 * h : 2 * h + 2]
+            dst = w_bf[:].rearrange("p u m t -> p m t u")
+            if h == 0:
+                nc.vector.tensor_copy(out=dst, in_=src)
+            else:
+                nc.scalar.activation(out=dst, in_=src, func=COPY)
+            w_q.append(
+                quantise(f"w{h}", w_bf[:].rearrange("p u m t -> p (u m t)"), E5M2, f"w_codes{h}", f"w_plane{h}")
+            )
+
+        hb_bf = first_layer("b", ub_q, 1)
+
+        ua_bf = sb.tile([P, HALF, PACK], BF16, name="ua_bf", tag="rounded1", align_bytes=64)
+        gather(ua_bf, 0, xa_01[:, 0, :], list_a)
+        gather(ua_bf, 1, xa_01[:, 1, :], list_a)
+        gather(ua_bf, 2, xa_2[:], list_a)
+
+        hb_q = quantise("hb", hb_bf, E5M2, "codes1", "shared_plane")
         p_b = ps.tile([P, GROUPS, HALF], F32, name="p_b")
-        two_layers("b", [xb_raw[:, t, :] for t in range(PACK)], list_b, [p_b[:, g, :] for g in range(GROUPS)], 1, ("codes0", "codes1"))
+        second_layer(hb_q, [p_b[:, g, :] for g in range(GROUPS)])
 
-        p_a = [ps.tile([P, HALF], F32, name=f"p_a{g}") for g in range(GROUPS)]
-        two_layers("a", [xa_01[:, 0, :], xa_01[:, 1, :], xa_2[:], xa_3[:]], list_a, [bank[:] for bank in p_a], 2, ("codes1", "codes0"))
+        gather(ua_bf, 3, xa_3[:], list_a)
 
-        nc.vector.scalar_tensor_tensor(
-            out=res[:, :, HALF:J], in0=rs_raw[:, :, HALF:J], scalar=RES, in1=p_b[:], op0=MULT, op1=ADD
-        )
-        nc.vector.scalar_tensor_tensor(
-            out=res[:, :, HALF + 1 : J],
-            in0=p_b[:, :, 0 : HALF - 1],
-            scalar=LAG,
-            in1=res[:, :, HALF + 1 : J],
-            op0=MULT,
-            op1=ADD,
-        )
+        ua_q = quantise("ua", ua_bf[:].rearrange("p j t -> p (j t)"), E4M3, "codes1", "ua_plane")
+        ha_bf = first_layer("a", ua_q, 2)
+
+        out_rows = out.rearrange("(g p) j -> p g j", p=P)
+        for g in range(GROUPS):
+            nc.vector.scalar_tensor_tensor(
+                out=res[:, g, HALF:J], in0=rs_raw[:, g, HALF:J], scalar=RES, in1=p_b[:, g, :], op0=MULT, op1=ADD
+            )
+        for g in range(GROUPS):
+            nc.vector.scalar_tensor_tensor(
+                out=res[:, g, HALF + 1 : J],
+                in0=p_b[:, g, 0 : HALF - 1],
+                scalar=LAG,
+                in1=res[:, g, HALF + 1 : J],
+                op0=MULT,
+                op1=ADD,
+            )
         nc.sync.dma_start(out=out_rows[:, :, EARLY:J], in_=res[:, :, EARLY:J])
+
+        ha_q = quantise("ha", ha_bf, E5M2, "codes0", "ha_plane")
+        p_a = [ps.tile([P, HALF], F32, name=f"p_a{g}") for g in range(GROUPS)]
+        second_layer(ha_q, [bank[:] for bank in p_a])
 
         for g in range(GROUPS):
             nc.vector.scalar_tensor_tensor(

from contextlib import ExitStack

import concourse.mybir as mybir

K, T, S, R, N, J = 512, 1024, 512, 512, 256, 256
FLOPS = 2 * K * R * J + 2 * R * N * J

F32 = mybir.dt.float32
BF16 = mybir.dt.bfloat16
I32 = mybir.dt.int32
U32 = mybir.dt.uint32
U16 = mybir.dt.uint16
U8 = mybir.dt.uint8
E4M3 = mybir.dt.float8_e4m3fn_x4
E5M2 = mybir.dt.float8_e5m2_x4
E2M1 = mybir.dt.float4_e2m1fn_x4
MULT = mybir.AluOpType.mult
ADD = mybir.AluOpType.add
COPY = mybir.ActivationFunctionType.Copy
RELU = mybir.ActivationFunctionType.Relu

P = 128
PACK = 4
HALF = 128
GROUPS = N // P
LAG = -0.7
RES = 0.5
EARLY = HALF + 8


def tile_list_joined_plain_lagged_kernel(tc, xa, xb, w, wb_words, wb_scales, rs, offs, offs2, out):
    nc = tc.nc
    with ExitStack() as ctx:
        sb = ctx.enter_context(tc.tile_pool(name="sb", bufs=1))
        ps = ctx.enter_context(tc.psum_pool(name="ps", bufs=1))

        list_a = sb.tile([P, HALF // 16], U16, name="list_a")
        list_b = sb.tile([P, HALF // 16], U16, name="list_b")
        w_raw = sb.tile([P, PACK, R], F32, name="w_raw")
        xb_raw = sb.tile([P, PACK, S], F32, name="xb_raw")
        xa_01 = sb.tile([P, 2, T], F32, name="xa_01")
        xa_2 = sb.tile([P, T], F32, name="xa_2", tag="shared_plane", align_bytes=64)
        xa_3 = sb.tile([P, T], F32, name="xa_3")
        wb_codes = sb.tile([P, 2 * N], U8, name="wb_codes", align_bytes=64)
        wb_plane = sb.tile([P, N], U8, name="wb_plane", align_bytes=64)
        rs_raw = sb.tile([P, GROUPS, J], F32, name="rs_raw")
        res = sb.tile([P, GROUPS, J], F32, name="res")

        nc.vector.memset(wb_plane[:].bitcast(U32), 0)
        xa_rows = xa.rearrange("(p t) c -> p t c", t=PACK)

        def load_w():
            nc.sync.dma_start(out=w_raw[:], in_=w.rearrange("(p t) r -> p t r", t=PACK))

        def load_xb():
            nc.sync.dma_start(out=xb_raw[:], in_=xb.rearrange("(p t) c -> p t c", t=PACK))

        def load_lists():
            nc.sync.dma_start(list_b[:], offs2)
            nc.sync.dma_start(list_a[:], offs)

        def load_scales():
            for q in range(4):
                nc.sync.dma_start(
                    out=wb_plane[32 * q : 32 * q + 4, :].bitcast(I32),
                    in_=wb_scales[0, 4 * q : 4 * q + 4, :].bitcast(I32),
                )

        load_xb()
        load_lists()
        load_scales()
        load_w()
        nc.sync.dma_start(out=xa_01[:], in_=xa_rows[:, 0:2, :])
        nc.sync.dma_start(out=wb_codes[:].bitcast(I32), in_=wb_words[0].bitcast(I32))
        nc.sync.dma_start(out=xa_2[:], in_=xa_rows[:, 2, :])
        nc.sync.dma_start(out=xa_3[:], in_=xa_rows[:, 3, :])
        nc.sync.dma_start(out=rs_raw[:], in_=rs.rearrange("(g p) j -> p g j", p=P))

        def quantise(name, values, fmt, codes_tag, plane_tag):
            width = values.shape[1] // PACK
            codes = sb.tile([P, width], U32, name=f"{name}_codes", tag=codes_tag, align_bytes=64)
            plane = sb.tile([P, width], U8, name=f"{name}_plane", tag=plane_tag, align_bytes=64)
            nc.vector.quantize_mx(out=codes[:].bitcast(fmt), scales=plane[:], in_=values)
            return codes, plane

        def gather(u_bf, t, window, offsets):
            nc.vector.tensor_copy(out=u_bf[:, :, t], in_=window.indirect(offsets[:]))

        def first_layer(name, u_q, parts):
            width = PACK // parts
            banks = [ps.tile([P, width, HALF], F32, name=f"a_bank_{name}{i}") for i in range(parts)]
            for u in range(PACK):
                cols = slice((u % 2) * P, (u % 2 + 1) * P)
                nc.tensor.matmul_mx(
                    out=banks[u // width][:, u % width, :],
                    lhsT=w_q[u // 2][0][:, cols].bitcast(E5M2),
                    lhsT_scale=w_q[u // 2][1][:, cols],
                    rhs=u_q[0][:].bitcast(E4M3),
                    rhs_scale=u_q[1][:],
                    start=True,
                    stop=True,
                )
            h_bf = sb.tile([P, HALF, PACK], BF16, name=f"h_bf_{name}", align_bytes=64)
            for i in range(parts):
                dst = h_bf[:, :, i * width : (i + 1) * width]
                src = banks[i][:].rearrange("p u j -> p j u")
                if i == parts - 1:
                    nc.scalar.activation(out=dst, in_=src, func=RELU)
                else:
                    nc.vector.tensor_scalar_max(out=dst, in0=src, scalar1=0.0)
            return h_bf[:].rearrange("p j t -> p (j t)")

        def second_layer(h_q, p_banks):
            for g in range(GROUPS):
                nc.tensor.matmul_mx(
                    out=p_banks[g],
                    lhsT=wb_codes[:, 2 * P * g : 2 * P * (g + 1)].bitcast(E2M1),
                    lhsT_scale=wb_plane[:, P * g : P * (g + 1)],
                    rhs=h_q[0][:].bitcast(E5M2),
                    rhs_scale=h_q[1][:],
                    start=True,
                    stop=True,
                )

        ub_bf = sb.tile([P, HALF, PACK], BF16, name="ub_bf", align_bytes=64)
        for t in range(PACK):
            gather(ub_bf, t, xb_raw[:, t, :], list_b)
        ub_q = quantise("ub", ub_bf[:].rearrange("p j t -> p (j t)"), E4M3, "codes0", "ub_plane")

        w_q = []
        for h in range(2):
            w_bf = sb.tile([P, 2, P, PACK], BF16, name=f"w_bf{h}", tag=f"rounded{h}", align_bytes=64)
            src = w_raw[:].rearrange("p t (m u) -> p m t u", u=PACK)[:, :, :, 2 * h : 2 * h + 2]
            dst = w_bf[:].rearrange("p u m t -> p m t u")
            if h == 0:
                nc.vector.tensor_copy(out=dst, in_=src)
            else:
                nc.scalar.activation(out=dst, in_=src, func=COPY)
            w_q.append(
                quantise(f"w{h}", w_bf[:].rearrange("p u m t -> p (u m t)"), E5M2, f"w_codes{h}", f"w_plane{h}")
            )

        hb_bf = first_layer("b", ub_q, 1)

        ua_bf = sb.tile([P, HALF, PACK], BF16, name="ua_bf", tag="rounded1", align_bytes=64)
        gather(ua_bf, 0, xa_01[:, 0, :], list_a)
        gather(ua_bf, 1, xa_01[:, 1, :], list_a)
        gather(ua_bf, 2, xa_2[:], list_a)

        hb_q = quantise("hb", hb_bf, E5M2, "codes1", "shared_plane")
        p_b = ps.tile([P, GROUPS, HALF], F32, name="p_b")
        second_layer(hb_q, [p_b[:, g, :] for g in range(GROUPS)])

        gather(ua_bf, 3, xa_3[:], list_a)

        ua_q = quantise("ua", ua_bf[:].rearrange("p j t -> p (j t)"), E4M3, "codes1", "ua_plane")
        ha_bf = first_layer("a", ua_q, 2)

        out_rows = out.rearrange("(g p) j -> p g j", p=P)
        for g in range(GROUPS):
            nc.vector.scalar_tensor_tensor(
                out=res[:, g, HALF:J], in0=rs_raw[:, g, HALF:J], scalar=RES, in1=p_b[:, g, :], op0=MULT, op1=ADD
            )
        for g in range(GROUPS):
            nc.vector.scalar_tensor_tensor(
                out=res[:, g, HALF + 1 : J],
                in0=p_b[:, g, 0 : HALF - 1],
                scalar=LAG,
                in1=res[:, g, HALF + 1 : J],
                op0=MULT,
                op1=ADD,
            )
        nc.sync.dma_start(out=out_rows[:, :, EARLY:J], in_=res[:, :, EARLY:J])

        ha_q = quantise("ha", ha_bf, E5M2, "codes0", "ha_plane")
        p_a = [ps.tile([P, HALF], F32, name=f"p_a{g}") for g in range(GROUPS)]
        second_layer(ha_q, [bank[:] for bank in p_a])

        for g in range(GROUPS):
            nc.vector.scalar_tensor_tensor(
                out=res[:, g, 0:HALF], in0=rs_raw[:, g, 0:HALF], scalar=RES, in1=p_a[g][:], op0=MULT, op1=ADD
            )
        for g in range(GROUPS):
            nc.vector.scalar_tensor_tensor(
                out=res[:, g, 1 : HALF + 1],
                in0=p_a[g][:],
                scalar=LAG,
                in1=res[:, g, 1 : HALF + 1],
                op0=MULT,
                op1=ADD,
            )
            queue = nc.sync if g == 0 else nc.scalar
            queue.dma_start(out=out_rows[:, g, 0:EARLY], in_=res[:, g, 0:EARLY])
